import numpy as np
import ml_dtypes


def mxq(x, axis, fmt="e4m3"):
    dtype, down = {"e4m3": (ml_dtypes.float8_e4m3fn, 7), "e5m2": (ml_dtypes.float8_e5m2, 14)}[fmt]
    v = np.moveaxis(np.asarray(x, np.float32).astype(ml_dtypes.bfloat16).astype(np.float64), axis, -1)
    blocks = v.reshape(v.shape[:-1] + (-1, 32))
    amax = np.abs(blocks).max(-1, keepdims=True)
    byte = np.maximum(np.where(amax > 0, np.frexp(amax)[1] - 1 + 127, 0) - down, 1)
    scale = np.exp2(byte - 127.0)
    codes = (blocks / scale).astype(np.float32).astype(dtype).astype(np.float64)
    return np.moveaxis((codes * scale).reshape(v.shape), -1, axis)


WIDE = False


def mx_kscale(k):
    if not WIDE:
        return np.ones(k)
    levels = np.array([30, -30])
    if k % 512:
        return np.exp2(np.random.permutation(np.resize(levels, k // 32))).repeat(32)
    a = np.empty((k // 512, 16))
    for p in range(k // 512):
        a[p, :8] = np.random.permutation(np.resize(levels, 8))
        for g in range(8):
            far = levels[np.abs(levels - a[p, g]) >= 10]
            a[p, g + 8] = far[np.random.randint(len(far))]
    return np.exp2(a.ravel()).repeat(32)


def f64(x):
    return np.asarray(x).astype(np.float64)


def striped(idx):
    return np.tile(np.asarray(idx).reshape(-1, 16).T, (8, 1)).astype(np.uint16)


def unstriped(offs):
    return offs[:16].T.reshape(-1).astype(np.int64)


E2M1 = np.array([0.0, 0.5, 1.0, 1.5, 2.0, 3.0, 4.0, 6.0, -0.0, -0.5, -1.0, -1.5, -2.0, -3.0, -4.0, -6.0])


def pack_weight(w, fmt):
    k, n = w.shape
    w = f64(np.asarray(w, np.float32).astype(ml_dtypes.bfloat16)).reshape(k // 32, 32, n)
    amax = np.abs(w).max(1)
    if fmt == "e4m3":
        byte = np.frexp(amax)[1] - 1 + 127 - 7
    else:
        mant, ex = np.frexp(amax / 6.0)
        byte = np.where(mant > 0.5, ex, ex - 1) + 127
    byte = np.clip(np.where(amax > 0, byte, 1), 1, 254)
    scaled = (w * np.exp2(127.0 - byte)[:, None, :]).reshape(k, n).astype(np.float32)
    by_word = np.ascontiguousarray(scaled.reshape(k // 512, 128, 4, n).transpose(0, 1, 3, 2))
    if fmt == "e4m3":
        words = by_word.astype(ml_dtypes.float8_e4m3fn).view(np.uint8)
    else:
        c = by_word.astype(ml_dtypes.float4_e2m1fn).view(np.uint8) & 0xF
        words = (c[..., 0::2] | (c[..., 1::2] << 4)).reshape(k // 512, 128, 2 * n)
    return np.ascontiguousarray(words), np.ascontiguousarray(byte.astype(np.uint8).reshape(k // 512, 16, n))


def unpack_weight(words, scales, fmt):
    g, _, n = scales.shape
    words = np.ascontiguousarray(words).reshape(g, 128, n, -1)
    if fmt == "e4m3":
        vals = words.view(ml_dtypes.float8_e4m3fn).astype(np.float64)
    else:
        nib = np.empty((g, 128, n, 4), np.uint8)
        nib[..., 0::2] = words & 0xF
        nib[..., 1::2] = words >> 4
        vals = E2M1[nib]
    vals = vals * np.repeat(np.exp2(scales.astype(np.float64) - 127.0), 8, axis=1)[..., None]
    return vals.transpose(0, 1, 3, 2).reshape(g * 512, n)


K, R, N, T, J = 512, 512, 512, 1024, 512


def setup_inputs():
    n = np.random.standard_normal
    idx = np.random.permutation(T)[:J]
    fn = mx_kscale(N)
    fr = mx_kscale(R)
    wdp = pack_weight(n((N, R)) * 1 / np.sqrt(N) * fn[:, None], "e2m1")
    wap = pack_weight(n((R, K)) * 1 / np.sqrt(R) / fr[:, None], "e4m3")
    wup = pack_weight(n((R, K)) * 1 / np.sqrt(R) / fr[:, None], "e2m1")
    return {
        "g": (n((N, T)) * np.exp(0.5 * n((1, T))) / fn[:, None]).astype(np.float32),
        "wd_words": wdp[0],
        "wd_scales": wdp[1],
        "va": (n((R, T)) * fr[:, None]).astype(np.float32),
        "u": (n((R, T)) * fr[:, None]).astype(np.float32),
        "wa_words": wap[0],
        "wa_scales": wap[1],
        "wu_words": wup[0],
        "wu_scales": wup[1],
        "offs": striped(idx),
    }


def reference(g, wd_words, wd_scales, va, u, wa_words, wa_scales, wu_words, wu_scales, offs):
    idx = unstriped(offs)
    wdu = unpack_weight(wd_words, wd_scales, "e2m1")
    wau = unpack_weight(wa_words, wa_scales, "e4m3")
    wuu = unpack_weight(wu_words, wu_scales, "e2m1")
    gidxq = mxq(f64(g)[:, idx], 0, "e5m2")
    dh = wdu.T @ gidxq
    da = dh * f64(u)[:, idx]
    du = dh * f64(va)[:, idx]
    daq = mxq(da, 0, "e5m2")
    duq = mxq(du, 0, "e4m3")
    y = wau.T @ daq + wuu.T @ duq
    return y

@@ -1,0 +1,192 @@
+from contextlib import ExitStack
+
+import concourse.mybir as mybir
+
+K, R, N, T, J = 512, 512, 512, 1024, 512
+FLOPS = 2 * N * R * J + 2 * 2 * R * K * J
+
+F32 = mybir.dt.float32
+BF16 = mybir.dt.bfloat16
+I32 = mybir.dt.int32
+U32 = mybir.dt.uint32
+U16 = mybir.dt.uint16
+U8 = mybir.dt.uint8
+E4M3 = mybir.dt.float8_e4m3fn_x4
+E5M2 = mybir.dt.float8_e5m2_x4
+E2M1 = mybir.dt.float4_e2m1fn_x4
+MULT = mybir.AluOpType.mult
+COPY = mybir.ActivationFunctionType.Copy
+
+P = 128
+PACK = 4
+CHUNK = 128
+CHUNKS = J // CHUNK
+GROUP = 16
+LINE = 4
+
+
+def tile_list_product_unit_back_kernel(
+    tc, g, wd_words, wd_scales, va, u, wa_words, wa_scales, wu_words, wu_scales, offs, out
+):
+    nc = tc.nc
+    with ExitStack() as ctx:
+        keep = ctx.enter_context(tc.tile_pool(name="keep", bufs=1))
+        psum = ctx.enter_context(tc.psum_pool(name="psum", bufs=1))
+
+        offsets = keep.tile([P, J // GROUP], U16, name="offsets")
+
+        def planes(name):
+            return [keep.tile([P, T], F32, name=f"{name}{t}") for t in range(PACK)]
+
+        g_rows, u_rows, va_rows = planes("g_rows"), planes("u_rows"), planes("va_rows")
+
+        def load_plane(tiles, src, t):
+            nc.sync.dma_start(out=tiles[t][:], in_=src.rearrange("(p t) x -> p t x", t=PACK)[:, t, :])
+
+        def scale_tile(name):
+            tile = keep.tile([P, 512], U8, name=name, align_bytes=64)
+            nc.gpsimd.memset(tile[:].bitcast(I32), 0)
+            return tile
+
+        def load_scales(tile, src):
+            for q in range(4):
+                nc.sync.dma_start(
+                    out=tile[32 * q : 32 * q + 4, :].bitcast(I32),
+                    in_=src[0, 4 * q : 4 * q + 4, :].bitcast(I32),
+                )
+
+        def listed(tile, j0, j1):
+            return tile[:].indirect(offsets[:, j0 // GROUP : j1 // GROUP])
+
+        def gather_scalar(dst, tiles, t, j0, j1):
+            nc.scalar.activation(out=dst[:, t, j0:j1], in_=listed(tiles[t], j0, j1), func=COPY)
+
+        def gather_vector(dst, tiles, t, j0, j1):
+            nc.vector.tensor_copy(out=dst[:, t, j0:j1], in_=listed(tiles[t], j0, j1))
+
+        wd_raw = keep.tile([P, R], U16, name="wd_raw")
+        wa_codes = keep.tile([P, K], U32, name="wa_codes", align_bytes=64)
+        wu_codes = keep.tile([P, K], U16, name="wu_codes", align_bytes=64)
+        wd_scale_raw = scale_tile("wd_scale_raw")
+        wa_scale = scale_tile("wa_scale")
+        wu_scale = scale_tile("wu_scale")
+
+        nc.sync.dma_start(offsets[:], offs)
+        load_plane(g_rows, g, 0)
+        load_plane(g_rows, g, 1)
+        nc.sync.dma_start(out=wd_raw[:].bitcast(I32), in_=wd_words[0].bitcast(I32))
+        load_scales(wd_scale_raw, wd_scales)
+        load_plane(g_rows, g, 2)
+        load_plane(g_rows, g, 3)
+        load_plane(u_rows, u, 0)
+        load_plane(u_rows, u, 1)
+        load_scales(wa_scale, wa_scales)
+        load_plane(u_rows, u, 2)
+        load_plane(u_rows, u, 3)
+        nc.sync.dma_start(
+            out=wa_codes[:].bitcast(I32), in_=wa_words[0].rearrange("p c b -> p (c b)").bitcast(I32)
+        )
+        load_plane(va_rows, va, 0)
+        load_plane(va_rows, va, 1)
+        load_scales(wu_scale, wu_scales)
+        load_plane(va_rows, va, 2)
+        load_plane(va_rows, va, 3)
+        nc.sync.dma_start(out=wu_codes[:].bitcast(I32), in_=wu_words[0].bitcast(I32))
+
+        g_picked = keep.tile([P, PACK, J], BF16, name="g_picked")
+        gather_scalar(g_picked, g_rows, 0, 0, J)
+        gather_vector(g_picked, g_rows, 1, 0, J)
+
+        wd_codes = keep.tile([P, PACK, P], U16, name="wd_codes", align_bytes=64)
+        wd_scale = keep.tile([P, PACK, P], U8, name="wd_scale", align_bytes=64)
+        nc.vector.tensor_copy(out=wd_codes[:], in_=wd_raw[:].rearrange("p (m t) -> p t m", t=PACK))
+        nc.vector.tensor_copy(out=wd_scale[:], in_=wd_scale_raw[:].rearrange("p (m t) -> p t m", t=PACK))
+
+        HALF = J // 2
+        gather_vector(g_picked, g_rows, 2, 0, J)
+        gather_scalar(g_picked, g_rows, 3, 0, HALF)
+        gather_vector(g_picked, g_rows, 3, HALF, J)
+        g_woven = [keep.tile([P, HALF, PACK], BF16, name=f"g_woven{h}", align_bytes=64) for h in range(2)]
+        g_codes = [keep.tile([P, HALF], U32, name=f"g_codes{h}", align_bytes=64) for h in range(2)]
+        g_scale = [keep.tile([P, HALF], U8, name=f"g_scale{h}", align_bytes=64) for h in range(2)]
+        for h in range(2):
+            nc.vector.tensor_copy(
+                out=g_woven[h][:].rearrange("p (c i) t -> p c t i", i=LINE),
+                in_=g_picked[:, :, h * HALF : (h + 1) * HALF].rearrange("p t (c i) -> p c t i", i=LINE),
+            )
+        for h in range(2):
+            nc.vector.quantize_mx(
+                out=g_codes[h][:].bitcast(E5M2),
+                scales=g_scale[h][:],
+                in_=g_woven[h][:].rearrange("p j t -> p (j t)"),
+            )
+
+        dh = [psum.tile([P, PACK, CHUNK], F32, name=f"dh{c}") for c in range(CHUNKS)]
+        for c in range(CHUNKS):
+            h, j0 = divmod(c * CHUNK, HALF)
+            for t in range(PACK):
+                nc.tensor.matmul_mx(
+                    out=dh[c][:, t, :],
+                    lhsT=wd_codes[:, t, :].bitcast(E2M1),
+                    lhsT_scale=wd_scale[:, t, :],
+                    rhs=g_codes[h][:, j0 : j0 + CHUNK].bitcast(E5M2),
+                    rhs_scale=g_scale[h][:, j0 : j0 + CHUNK],
+                    start=True,
+                    stop=True,
+                )
+
+        y = [psum.tile([P, K // P, CHUNK], F32, name=f"y{c}") for c in range(CHUNKS)]
+        out_view = out.rearrange("(a p) j -> p a j", p=P)
+
+        def branch(name, rows, fmt, w_codes, w_fmt, w_scale, first):
+            picked = keep.tile([P, PACK, J], F32, name=f"{name}_picked")
+            for t in range(PACK - 2):
+                gather_scalar(picked, rows, t, 0, J)
+            if first:
+                gather_scalar(picked, rows, PACK - 2, 0, J)
+            else:
+                gather_scalar(picked, rows, PACK - 2, 0, HALF)
+                gather_vector(picked, rows, PACK - 2, HALF, J)
+            for c in range(CHUNKS):
+                gather_scalar(picked, rows, PACK - 1, c * CHUNK, (c + 1) * CHUNK)
+            woven = [
+                keep.tile([P, CHUNK, PACK], BF16, name=f"{name}_woven{c}", align_bytes=64) for c in range(CHUNKS)
+            ]
+            codes = [keep.tile([P, CHUNK], U32, name=f"{name}_codes{c}", align_bytes=64) for c in range(CHUNKS)]
+            scale = [keep.tile([P, CHUNK], U8, name=f"{name}_scale{c}", align_bytes=64) for c in range(CHUNKS)]
+
+            def multiply(c):
+                nc.vector.tensor_tensor(
+                    out=woven[c][:].rearrange("p (c i) t -> p c t i", i=LINE),
+                    in0=dh[c][:].rearrange("p t (c i) -> p c t i", i=LINE),
+                    in1=picked[:, :, c * CHUNK : (c + 1) * CHUNK].rearrange("p t (c i) -> p c t i", i=LINE),
+                    op=MULT,
+                )
+
+            def finish(c):
+                nc.vector.quantize_mx(
+                    out=codes[c][:].bitcast(fmt), scales=scale[c][:], in_=woven[c][:].rearrange("p j t -> p (j t)")
+                )
+                for a in range(K // P):
+                    nc.tensor.matmul_mx(
+                        out=y[c][:, a, :],
+                        lhsT=w_codes[:, a * P : (a + 1) * P].bitcast(w_fmt),
+                        lhsT_scale=w_scale[:, a * P : (a + 1) * P],
+                        rhs=codes[c][:].bitcast(fmt),
+                        rhs_scale=scale[c][:],
+                        start=(first and a == 0),
+                        stop=(not first and a == K // P - 1),
+                    )
+                if not first:
+                    result = keep.tile([P, K // P, CHUNK], F32, name=f"result{c}")
+                    nc.scalar.copy(out=result[:], in_=y[c][:])
+                    nc.sync.dma_start(out=out_view[:, :, c * CHUNK : (c + 1) * CHUNK], in_=result[:])
+
+            multiply(0)
+            for c in range(1, CHUNKS):
+                multiply(c)
+                finish(c - 1)
+            finish(CHUNKS - 1)
+
+        branch("da", u_rows, E5M2, wa_codes, E4M3, wa_scale, True)
+        branch("du", va_rows, E4M3, wu_codes, E2M1, wu_scale, False)

@@ -80,17 +80,17 @@ def tile_list_product_unit_back_kernel(
         load_plane(g_rows, g, 3)
         load_plane(u_rows, u, 0)
         load_plane(u_rows, u, 1)
-        load_scales(wa_scale, wa_scales)
+        load_scales(wu_scale, wu_scales)
         load_plane(u_rows, u, 2)
         load_plane(u_rows, u, 3)
+        load_plane(va_rows, va, 0)
+        load_plane(va_rows, va, 1)
+        load_plane(va_rows, va, 2)
+        load_plane(va_rows, va, 3)
+        load_scales(wa_scale, wa_scales)
         nc.sync.dma_start(
             out=wa_codes[:].bitcast(I32), in_=wa_words[0].rearrange("p c b -> p (c b)").bitcast(I32)
         )
-        load_plane(va_rows, va, 0)
-        load_plane(va_rows, va, 1)
-        load_scales(wu_scale, wu_scales)
-        load_plane(va_rows, va, 2)
-        load_plane(va_rows, va, 3)
         nc.sync.dma_start(out=wu_codes[:].bitcast(I32), in_=wu_words[0].bitcast(I32))
 
         g_picked = keep.tile([P, PACK, J], BF16, name="g_picked")
@@ -135,58 +135,104 @@ def tile_list_product_unit_back_kernel(
                     stop=True,
                 )
 
-        y = [psum.tile([P, K // P, CHUNK], F32, name=f"y{c}") for c in range(CHUNKS)]
         out_view = out.rearrange("(a p) j -> p a j", p=P)
+        K_TILES = K // P
 
-        def branch(name, rows, fmt, w_codes, w_fmt, w_scale, first):
-            picked = keep.tile([P, PACK, J], F32, name=f"{name}_picked")
-            for t in range(PACK - 2):
-                gather_scalar(picked, rows, t, 0, J)
-            if first:
-                gather_scalar(picked, rows, PACK - 2, 0, J)
-            else:
-                gather_scalar(picked, rows, PACK - 2, 0, HALF)
-                gather_vector(picked, rows, PACK - 2, HALF, J)
-            for c in range(CHUNKS):
-                gather_scalar(picked, rows, PACK - 1, c * CHUNK, (c + 1) * CHUNK)
+        def operand_tiles(name):
             woven = [
                 keep.tile([P, CHUNK, PACK], BF16, name=f"{name}_woven{c}", align_bytes=64) for c in range(CHUNKS)
             ]
             codes = [keep.tile([P, CHUNK], U32, name=f"{name}_codes{c}", align_bytes=64) for c in range(CHUNKS)]
             scale = [keep.tile([P, CHUNK], U8, name=f"{name}_scale{c}", align_bytes=64) for c in range(CHUNKS)]
+            return woven, codes, scale
 
-            def multiply(c):
-                nc.vector.tensor_tensor(
-                    out=woven[c][:].rearrange("p (c i) t -> p c t i", i=LINE),
-                    in0=dh[c][:].rearrange("p t (c i) -> p c t i", i=LINE),
-                    in1=picked[:, :, c * CHUNK : (c + 1) * CHUNK].rearrange("p t (c i) -> p c t i", i=LINE),
-                    op=MULT,
-                )
+        def multiply(picked, woven, c):
+            nc.vector.tensor_tensor(
+                out=woven[c][:].rearrange("p (c i) t -> p c t i", i=LINE),
+                in0=dh[c][:].rearrange("p t (c i) -> p c t i", i=LINE),
+                in1=picked[:, :, c * CHUNK : (c + 1) * CHUNK].rearrange("p t (c i) -> p c t i", i=LINE),
+                op=MULT,
+            )
 
-            def finish(c):
-                nc.vector.quantize_mx(
-                    out=codes[c][:].bitcast(fmt), scales=scale[c][:], in_=woven[c][:].rearrange("p j t -> p (j t)")
-                )
-                for a in range(K // P):
+        def quantise(woven, codes, scale, fmt, c):
+            nc.vector.quantize_mx(
+                out=codes[c][:].bitcast(fmt), scales=scale[c][:], in_=woven[c][:].rearrange("p j t -> p (j t)")
+            )
+
+        u_picked = keep.tile([P, PACK, J], F32, name="u_picked")
+        for t in range(PACK - 2):
+            gather_scalar(u_picked, u_rows, t, 0, J)
+        gather_vector(u_picked, u_rows, PACK - 2, 0, J)
+        gather_vector(u_picked, u_rows, PACK - 1, 0, CHUNK)
+        for c in range(1, CHUNKS):
+            gather_scalar(u_picked, u_rows, PACK - 1, c * CHUNK, (c + 1) * CHUNK)
+        da_woven, da_codes, da_scale = operand_tiles("da")
+        multiply(u_picked, da_woven, 0)
+        for c in range(1, CHUNKS):
+            multiply(u_picked, da_woven, c)
+            quantise(da_woven, da_codes, da_scale, E5M2, c - 1)
+        quantise(da_woven, da_codes, da_scale, E5M2, CHUNKS - 1)
+
+        va_picked = keep.tile([P, PACK, J], F32, name="va_picked")
+        for t in range(PACK - 2):
+            gather_scalar(va_picked, va_rows, t, 0, J)
+        gather_scalar(va_picked, va_rows, PACK - 2, 0, HALF)
+        gather_vector(va_picked, va_rows, PACK - 2, HALF, J)
+        for c in range(CHUNKS):
+            gather_scalar(va_picked, va_rows, PACK - 1, c * CHUNK, (c + 1) * CHUNK)
+        du_woven, du_codes, du_scale = operand_tiles("du")
+
+        def passes(c, w_codes, w_fmt, w_scale, codes, fmt, scale, first):
+            for bank, k_tiles in y[c]:
+                for a in k_tiles:
                     nc.tensor.matmul_mx(
-                        out=y[c][:, a, :],
+                        out=bank[:, a - k_tiles.start, :],
                         lhsT=w_codes[:, a * P : (a + 1) * P].bitcast(w_fmt),
                         lhsT_scale=w_scale[:, a * P : (a + 1) * P],
                         rhs=codes[c][:].bitcast(fmt),
                         rhs_scale=scale[c][:],
-                        start=(first and a == 0),
-                        stop=(not first and a == K // P - 1),
+                        start=(first and a == k_tiles.start),
+                        stop=(not first and a == k_tiles.stop - 1),
                     )
-                if not first:
-                    result = keep.tile([P, K // P, CHUNK], F32, name=f"result{c}")
-                    nc.scalar.copy(out=result[:], in_=y[c][:])
-                    nc.sync.dma_start(out=out_view[:, :, c * CHUNK : (c + 1) * CHUNK], in_=result[:])
 
-            multiply(0)
-            for c in range(1, CHUNKS):
-                multiply(c)
-                finish(c - 1)
-            finish(CHUNKS - 1)
+        y = {}
+        res = {}
 
-        branch("da", u_rows, E5M2, wa_codes, E4M3, wa_scale, True)
-        branch("du", va_rows, E4M3, wu_codes, E2M1, wu_scale, False)
+        def open_sums(c, parts, tag=None):
+            width = K_TILES // parts
+            y[c] = [
+                (
+                    psum.tile([P, width, CHUNK], F32, name=f"y{c}_{n}", tag=tag or f"y{c}_{n}"),
+                    range(n * width, (n + 1) * width),
+                )
+                for n in range(parts)
+            ]
+            passes(c, wa_codes, E4M3, wa_scale, da_codes, E5M2, da_scale, True)
+
+        def close_sums(c):
+            quantise(du_woven, du_codes, du_scale, E4M3, c)
+            passes(c, wu_codes, E2M1, wu_scale, du_codes, E4M3, du_scale, False)
+
+        def store(c, copies):
+            result = keep.tile([P, K_TILES, CHUNK], F32, name=f"result{c}")
+            res[c] = result
+            for (bank, k_tiles), copy in zip(y[c], copies):
+                copy(out=result[:, k_tiles.start : k_tiles.stop, :], in_=bank[:])
+            nc.sync.dma_start(out=out_view[:, :, c * CHUNK : (c + 1) * CHUNK], in_=result[:])
+
+        open_sums(0, 1)
+        open_sums(1, 1)
+        open_sums(3, 2)
+        multiply(va_picked, du_woven, 0)
+        multiply(va_picked, du_woven, 1)
+        close_sums(0)
+        store(0, [nc.scalar.copy])
+        multiply(va_picked, du_woven, 2)
+        open_sums(2, 1, tag="dh2")
+        close_sums(1)
+        store(1, [nc.scalar.copy])
+        multiply(va_picked, du_woven, 3)
+        close_sums(2)
+        close_sums(3)
+        store(2, [nc.vector.tensor_copy])
+        store(3, [nc.scalar.copy, nc.vector.tensor_copy])

@@ -65,7 +65,12 @@ def tile_list_product_unit_back_kernel(
             nc.vector.tensor_copy(out=dst[:, t, j0:j1], in_=listed(tiles[t], j0, j1))
 
         wd_raw = keep.tile([P, R], U16, name="wd_raw")
-        wa_codes = keep.tile([P, K], U32, name="wa_codes", align_bytes=64)
+        wa_halves = [keep.tile([P, K // 2], U32, name=f"wa_codes{h}", align_bytes=64) for h in range(2)]
+        wa_view = wa_words[0].rearrange("p c b -> p (c b)").bitcast(I32)
+
+        def load_wa(h):
+            nc.sync.dma_start(out=wa_halves[h][:].bitcast(I32), in_=wa_view[:, h * (K // 2) : (h + 1) * (K // 2)])
+
         wu_codes = keep.tile([P, K], U16, name="wu_codes", align_bytes=64)
         wd_scale_raw = scale_tile("wd_scale_raw")
         wa_scale = scale_tile("wa_scale")
@@ -80,17 +85,16 @@ def tile_list_product_unit_back_kernel(
         load_plane(g_rows, g, 3)
         load_plane(u_rows, u, 0)
         load_plane(u_rows, u, 1)
-        load_scales(wu_scale, wu_scales)
+        load_scales(wa_scale, wa_scales)
         load_plane(u_rows, u, 2)
         load_plane(u_rows, u, 3)
         load_plane(va_rows, va, 0)
         load_plane(va_rows, va, 1)
         load_plane(va_rows, va, 2)
+        load_wa(0)
         load_plane(va_rows, va, 3)
-        load_scales(wa_scale, wa_scales)
-        nc.sync.dma_start(
-            out=wa_codes[:].bitcast(I32), in_=wa_words[0].rearrange("p c b -> p (c b)").bitcast(I32)
-        )
+        load_wa(1)
+        load_scales(wu_scale, wu_scales)
         nc.sync.dma_start(out=wu_codes[:].bitcast(I32), in_=wu_words[0].bitcast(I32))
 
         g_picked = keep.tile([P, PACK, J], BF16, name="g_picked")
@@ -146,11 +150,11 @@ def tile_list_product_unit_back_kernel(
             scale = [keep.tile([P, CHUNK], U8, name=f"{name}_scale{c}", align_bytes=64) for c in range(CHUNKS)]
             return woven, codes, scale
 
-        def multiply(picked, woven, c):
+        def multiply(picked, woven, c, t0=0, t1=PACK):
             nc.vector.tensor_tensor(
-                out=woven[c][:].rearrange("p (c i) t -> p c t i", i=LINE),
-                in0=dh[c][:].rearrange("p t (c i) -> p c t i", i=LINE),
-                in1=picked[:, :, c * CHUNK : (c + 1) * CHUNK].rearrange("p t (c i) -> p c t i", i=LINE),
+                out=woven[c][:, :, t0:t1].rearrange("p (c i) t -> p c t i", i=LINE),
+                in0=dh[c][:, t0:t1, :].rearrange("p t (c i) -> p c t i", i=LINE),
+                in1=picked[:, t0:t1, c * CHUNK : (c + 1) * CHUNK].rearrange("p t (c i) -> p c t i", i=LINE),
                 op=MULT,
             )
 
@@ -174,65 +178,70 @@ def tile_list_product_unit_back_kernel(
         quantise(da_woven, da_codes, da_scale, E5M2, CHUNKS - 1)
 
         va_picked = keep.tile([P, PACK, J], F32, name="va_picked")
-        for t in range(PACK - 2):
+        for t in range(PACK - 1):
             gather_scalar(va_picked, va_rows, t, 0, J)
-        gather_scalar(va_picked, va_rows, PACK - 2, 0, HALF)
-        gather_vector(va_picked, va_rows, PACK - 2, HALF, J)
         for c in range(CHUNKS):
             gather_scalar(va_picked, va_rows, PACK - 1, c * CHUNK, (c + 1) * CHUNK)
         du_woven, du_codes, du_scale = operand_tiles("du")
 
-        def passes(c, w_codes, w_fmt, w_scale, codes, fmt, scale, first):
-            for bank, k_tiles in y[c]:
-                for a in k_tiles:
+        for c in range(CHUNKS):
+            multiply(va_picked, du_woven, c, 0, 2)
+
+        def part(name, k_tiles, chunks):
+            bank = psum.tile([P, len(k_tiles), len(chunks) * CHUNK], F32, name=name)
+            return bank, k_tiles, chunks
+
+        parts = [
+            part("y0", range(K_TILES), range(0, 1)),
+            part("y1", range(K_TILES), range(1, 2)),
+            part("y23_low", range(0, 2), range(2, 4)),
+            part("y23_high", range(2, 4), range(2, 4)),
+        ]
+
+        def one_pass(c, a, lhsT, w_scale, rhs, rhs_scale, first):
+            for bank, k_tiles, chunks in parts:
+                if a in k_tiles and c in chunks:
+                    j0 = (c - chunks.start) * CHUNK
                     nc.tensor.matmul_mx(
-                        out=bank[:, a - k_tiles.start, :],
-                        lhsT=w_codes[:, a * P : (a + 1) * P].bitcast(w_fmt),
+                        out=bank[:, a - k_tiles.start, j0 : j0 + CHUNK],
+                        lhsT=lhsT,
                         lhsT_scale=w_scale[:, a * P : (a + 1) * P],
-                        rhs=codes[c][:].bitcast(fmt),
-                        rhs_scale=scale[c][:],
-                        start=(first and a == k_tiles.start),
-                        stop=(not first and a == k_tiles.stop - 1),
+                        rhs=rhs,
+                        rhs_scale=rhs_scale,
+                        start=(first and c == chunks.start and a == k_tiles.start),
+                        stop=(not first and c == chunks.stop - 1 and a == k_tiles.stop - 1),
                     )
 
-        y = {}
-        res = {}
-
-        def open_sums(c, parts, tag=None):
-            width = K_TILES // parts
-            y[c] = [
-                (
-                    psum.tile([P, width, CHUNK], F32, name=f"y{c}_{n}", tag=tag or f"y{c}_{n}"),
-                    range(n * width, (n + 1) * width),
-                )
-                for n in range(parts)
-            ]
-            passes(c, wa_codes, E4M3, wa_scale, da_codes, E5M2, da_scale, True)
+        for h in range(2):
+            for c in range(CHUNKS):
+                for n in range(2):
+                    lhsT = wa_halves[h][:, n * P : (n + 1) * P].bitcast(E4M3)
+                    one_pass(c, 2 * h + n, lhsT, wa_scale, da_codes[c][:].bitcast(E5M2), da_scale[c][:], True)
 
         def close_sums(c):
             quantise(du_woven, du_codes, du_scale, E4M3, c)
-            passes(c, wu_codes, E2M1, wu_scale, du_codes, E4M3, du_scale, False)
+            for a in range(K_TILES):
+                lhsT = wu_codes[:, a * P : (a + 1) * P].bitcast(E2M1)
+                one_pass(c, a, lhsT, wu_scale, du_codes[c][:].bitcast(E4M3), du_scale[c][:], False)
 
-        def store(c, copies):
-            result = keep.tile([P, K_TILES, CHUNK], F32, name=f"result{c}")
-            res[c] = result
-            for (bank, k_tiles), copy in zip(y[c], copies):
+        res = {}
+
+        def store(done, copies):
+            chunks = done[0][2]
+            result = keep.tile([P, K_TILES, len(chunks) * CHUNK], F32, name=f"result{chunks.start}")
+            res[chunks.start] = result
+            for (bank, k_tiles, chunks), copy in zip(done, copies):
                 copy(out=result[:, k_tiles.start : k_tiles.stop, :], in_=bank[:])
-            nc.sync.dma_start(out=out_view[:, :, c * CHUNK : (c + 1) * CHUNK], in_=result[:])
+            nc.sync.dma_start(out=out_view[:, :, chunks.start * CHUNK : chunks.stop * CHUNK], in_=result[:])
 
-        open_sums(0, 1)
-        open_sums(1, 1)
-        open_sums(3, 2)
-        multiply(va_picked, du_woven, 0)
-        multiply(va_picked, du_woven, 1)
+        multiply(va_picked, du_woven, 0, 2, 4)
+        multiply(va_picked, du_woven, 1, 2, 4)
         close_sums(0)
-        store(0, [nc.scalar.copy])
-        multiply(va_picked, du_woven, 2)
-        open_sums(2, 1, tag="dh2")
+        store(parts[0:1], [nc.scalar.copy])
+        multiply(va_picked, du_woven, 2, 2, 4)
         close_sums(1)
-        store(1, [nc.scalar.copy])
-        multiply(va_picked, du_woven, 3)
+        store(parts[1:2], [nc.scalar.copy])
+        multiply(va_picked, du_woven, 3, 2, 4)
         close_sums(2)
         close_sums(3)
-        store(2, [nc.vector.tensor_copy])
-        store(3, [nc.scalar.copy, nc.vector.tensor_copy])
+        store(parts[2:4], [nc.scalar.copy, nc.vector.tensor_copy])

from contextlib import ExitStack

import concourse.mybir as mybir

K, R, N, T, J = 512, 512, 512, 1024, 512
FLOPS = 2 * N * R * J + 2 * 2 * R * K * J

F32 = mybir.dt.float32
BF16 = mybir.dt.bfloat16
I32 = mybir.dt.int32
U32 = mybir.dt.uint32
U16 = mybir.dt.uint16
U8 = mybir.dt.uint8
E4M3 = mybir.dt.float8_e4m3fn_x4
E5M2 = mybir.dt.float8_e5m2_x4
E2M1 = mybir.dt.float4_e2m1fn_x4
MULT = mybir.AluOpType.mult
COPY = mybir.ActivationFunctionType.Copy

P = 128
PACK = 4
CHUNK = 128
CHUNKS = J // CHUNK
GROUP = 16
LINE = 4


def tile_list_product_unit_back_kernel(
    tc, g, wd_words, wd_scales, va, u, wa_words, wa_scales, wu_words, wu_scales, offs, out
):
    nc = tc.nc
    with ExitStack() as ctx:
        keep = ctx.enter_context(tc.tile_pool(name="keep", bufs=1))
        psum = ctx.enter_context(tc.psum_pool(name="psum", bufs=1))

        offsets = keep.tile([P, J // GROUP], U16, name="offsets")

        def planes(name):
            return [keep.tile([P, T], F32, name=f"{name}{t}") for t in range(PACK)]

        g_rows, u_rows, va_rows = planes("g_rows"), planes("u_rows"), planes("va_rows")

        def load_plane(tiles, src, t):
            nc.sync.dma_start(out=tiles[t][:], in_=src.rearrange("(p t) x -> p t x", t=PACK)[:, t, :])

        def scale_tile(name):
            tile = keep.tile([P, 512], U8, name=name, align_bytes=64)
            nc.gpsimd.memset(tile[:].bitcast(I32), 0)
            return tile

        def load_scales(tile, src):
            for q in range(4):
                nc.sync.dma_start(
                    out=tile[32 * q : 32 * q + 4, :].bitcast(I32),
                    in_=src[0, 4 * q : 4 * q + 4, :].bitcast(I32),
                )

        def listed(tile, j0, j1):
            return tile[:].indirect(offsets[:, j0 // GROUP : j1 // GROUP])

        def gather_scalar(dst, tiles, t, j0, j1):
            nc.scalar.activation(out=dst[:, t, j0:j1], in_=listed(tiles[t], j0, j1), func=COPY)

        def gather_vector(dst, tiles, t, j0, j1):
            nc.vector.tensor_copy(out=dst[:, t, j0:j1], in_=listed(tiles[t], j0, j1))

        wd_raw = keep.tile([P, R], U16, name="wd_raw")
        wa_halves = [keep.tile([P, K // 2], U32, name=f"wa_codes{h}", align_bytes=64) for h in range(2)]
        wa_view = wa_words[0].rearrange("p c b -> p (c b)").bitcast(I32)

        def load_wa(h):
            nc.sync.dma_start(out=wa_halves[h][:].bitcast(I32), in_=wa_view[:, h * (K // 2) : (h + 1) * (K // 2)])

        wu_codes = keep.tile([P, K], U16, name="wu_codes", align_bytes=64)
        wd_scale_raw = scale_tile("wd_scale_raw")
        wa_scale = scale_tile("wa_scale")
        wu_scale = scale_tile("wu_scale")

        nc.sync.dma_start(offsets[:], offs)
        load_plane(g_rows, g, 0)
        load_plane(g_rows, g, 1)
        nc.sync.dma_start(out=wd_raw[:].bitcast(I32), in_=wd_words[0].bitcast(I32))
        load_scales(wd_scale_raw, wd_scales)
        load_plane(g_rows, g, 2)
        load_plane(g_rows, g, 3)
        load_plane(u_rows, u, 0)
        load_plane(u_rows, u, 1)
        load_scales(wa_scale, wa_scales)
        load_plane(u_rows, u, 2)
        load_plane(u_rows, u, 3)
        load_plane(va_rows, va, 0)
        load_plane(va_rows, va, 1)
        load_plane(va_rows, va, 2)
        load_wa(0)
        load_plane(va_rows, va, 3)
        load_wa(1)
        load_scales(wu_scale, wu_scales)
        nc.sync.dma_start(out=wu_codes[:].bitcast(I32), in_=wu_words[0].bitcast(I32))

        g_picked = keep.tile([P, PACK, J], BF16, name="g_picked")
        gather_scalar(g_picked, g_rows, 0, 0, J)
        gather_vector(g_picked, g_rows, 1, 0, J)

        wd_codes = keep.tile([P, PACK, P], U16, name="wd_codes", align_bytes=64)
        wd_scale = keep.tile([P, PACK, P], U8, name="wd_scale", align_bytes=64)
        nc.vector.tensor_copy(out=wd_codes[:], in_=wd_raw[:].rearrange("p (m t) -> p t m", t=PACK))
        nc.vector.tensor_copy(out=wd_scale[:], in_=wd_scale_raw[:].rearrange("p (m t) -> p t m", t=PACK))

        HALF = J // 2
        gather_vector(g_picked, g_rows, 2, 0, J)
        gather_scalar(g_picked, g_rows, 3, 0, HALF)
        gather_vector(g_picked, g_rows, 3, HALF, J)
        g_woven = [keep.tile([P, HALF, PACK], BF16, name=f"g_woven{h}", align_bytes=64) for h in range(2)]
        g_codes = [keep.tile([P, HALF], U32, name=f"g_codes{h}", align_bytes=64) for h in range(2)]
        g_scale = [keep.tile([P, HALF], U8, name=f"g_scale{h}", align_bytes=64) for h in range(2)]
        for h in range(2):
            nc.vector.tensor_copy(
                out=g_woven[h][:].rearrange("p (c i) t -> p c t i", i=LINE),
                in_=g_picked[:, :, h * HALF : (h + 1) * HALF].rearrange("p t (c i) -> p c t i", i=LINE),
            )
        for h in range(2):
            nc.vector.quantize_mx(
                out=g_codes[h][:].bitcast(E5M2),
                scales=g_scale[h][:],
                in_=g_woven[h][:].rearrange("p j t -> p (j t)"),
            )

        dh = [psum.tile([P, PACK, CHUNK], F32, name=f"dh{c}") for c in range(CHUNKS)]
        for c in range(CHUNKS):
            h, j0 = divmod(c * CHUNK, HALF)
            for t in range(PACK):
                nc.tensor.matmul_mx(
                    out=dh[c][:, t, :],
                    lhsT=wd_codes[:, t, :].bitcast(E2M1),
                    lhsT_scale=wd_scale[:, t, :],
                    rhs=g_codes[h][:, j0 : j0 + CHUNK].bitcast(E5M2),
                    rhs_scale=g_scale[h][:, j0 : j0 + CHUNK],
                    start=True,
                    stop=True,
                )

        out_view = out.rearrange("(a p) j -> p a j", p=P)
        K_TILES = K // P

        def operand_tiles(name):
            woven = [
                keep.tile([P, CHUNK, PACK], BF16, name=f"{name}_woven{c}", align_bytes=64) for c in range(CHUNKS)
            ]
            codes = [keep.tile([P, CHUNK], U32, name=f"{name}_codes{c}", align_bytes=64) for c in range(CHUNKS)]
            scale = [keep.tile([P, CHUNK], U8, name=f"{name}_scale{c}", align_bytes=64) for c in range(CHUNKS)]
            return woven, codes, scale

        def multiply(picked, woven, c, t0=0, t1=PACK):
            nc.vector.tensor_tensor(
                out=woven[c][:, :, t0:t1].rearrange("p (c i) t -> p c t i", i=LINE),
                in0=dh[c][:, t0:t1, :].rearrange("p t (c i) -> p c t i", i=LINE),
                in1=picked[:, t0:t1, c * CHUNK : (c + 1) * CHUNK].rearrange("p t (c i) -> p c t i", i=LINE),
                op=MULT,
            )

        def quantise(woven, codes, scale, fmt, c):
            nc.vector.quantize_mx(
                out=codes[c][:].bitcast(fmt), scales=scale[c][:], in_=woven[c][:].rearrange("p j t -> p (j t)")
            )

        u_picked = keep.tile([P, PACK, J], F32, name="u_picked")
        for t in range(PACK - 2):
            gather_scalar(u_picked, u_rows, t, 0, J)
        gather_vector(u_picked, u_rows, PACK - 2, 0, J)
        gather_vector(u_picked, u_rows, PACK - 1, 0, CHUNK)
        for c in range(1, CHUNKS):
            gather_scalar(u_picked, u_rows, PACK - 1, c * CHUNK, (c + 1) * CHUNK)
        da_woven, da_codes, da_scale = operand_tiles("da")
        multiply(u_picked, da_woven, 0)
        for c in range(1, CHUNKS):
            multiply(u_picked, da_woven, c)
            quantise(da_woven, da_codes, da_scale, E5M2, c - 1)
        quantise(da_woven, da_codes, da_scale, E5M2, CHUNKS - 1)

        va_picked = keep.tile([P, PACK, J], F32, name="va_picked")
        for t in range(PACK - 1):
            gather_scalar(va_picked, va_rows, t, 0, J)
        for c in range(CHUNKS):
            gather_scalar(va_picked, va_rows, PACK - 1, c * CHUNK, (c + 1) * CHUNK)
        du_woven, du_codes, du_scale = operand_tiles("du")

        for c in range(CHUNKS):
            multiply(va_picked, du_woven, c, 0, 2)

        def part(name, k_tiles, chunks):
            bank = psum.tile([P, len(k_tiles), len(chunks) * CHUNK], F32, name=name)
            return bank, k_tiles, chunks

        parts = [
            part("y0", range(K_TILES), range(0, 1)),
            part("y1", range(K_TILES), range(1, 2)),
            part("y23_low", range(0, 2), range(2, 4)),
            part("y23_high", range(2, 4), range(2, 4)),
        ]

        def one_pass(c, a, lhsT, w_scale, rhs, rhs_scale, first):
            for bank, k_tiles, chunks in parts:
                if a in k_tiles and c in chunks:
                    j0 = (c - chunks.start) * CHUNK
                    nc.tensor.matmul_mx(
                        out=bank[:, a - k_tiles.start, j0 : j0 + CHUNK],
                        lhsT=lhsT,
                        lhsT_scale=w_scale[:, a * P : (a + 1) * P],
                        rhs=rhs,
                        rhs_scale=rhs_scale,
                        start=(first and c == chunks.start and a == k_tiles.start),
                        stop=(not first and c == chunks.stop - 1 and a == k_tiles.stop - 1),
                    )

        for h in range(2):
            for c in range(CHUNKS):
                for n in range(2):
                    lhsT = wa_halves[h][:, n * P : (n + 1) * P].bitcast(E4M3)
                    one_pass(c, 2 * h + n, lhsT, wa_scale, da_codes[c][:].bitcast(E5M2), da_scale[c][:], True)

        def close_sums(c):
            quantise(du_woven, du_codes, du_scale, E4M3, c)
            for a in range(K_TILES):
                lhsT = wu_codes[:, a * P : (a + 1) * P].bitcast(E2M1)
                one_pass(c, a, lhsT, wu_scale, du_codes[c][:].bitcast(E4M3), du_scale[c][:], False)

        res = {}

        def store(done, copies):
            chunks = done[0][2]
            result = keep.tile([P, K_TILES, len(chunks) * CHUNK], F32, name=f"result{chunks.start}")
            res[chunks.start] = result
            for (bank, k_tiles, chunks), copy in zip(done, copies):
                copy(out=result[:, k_tiles.start : k_tiles.stop, :], in_=bank[:])
            nc.sync.dma_start(out=out_view[:, :, chunks.start * CHUNK : chunks.stop * CHUNK], in_=result[:])

        multiply(va_picked, du_woven, 0, 2, 4)
        multiply(va_picked, du_woven, 1, 2, 4)
        close_sums(0)
        store(parts[0:1], [nc.scalar.copy])
        multiply(va_picked, du_woven, 2, 2, 4)
        close_sums(1)
        store(parts[1:2], [nc.scalar.copy])
        multiply(va_picked, du_woven, 3, 2, 4)
        close_sums(2)
        close_sums(3)
        store(parts[2:4], [nc.scalar.copy, nc.vector.tensor_copy])
